import numpy as np, ml_dtypes
CORES = [2,3,42,43,82,83,122,123]
N = 8
import mx_ref
NC = 512
BF = ml_dtypes.bfloat16
def setup_inputs(rng):
    def f(*shape):
        return mx_ref.flush((rng.standard_normal(shape, dtype=np.float32) * np.exp2(rng.integers(-2, 3, shape[:-1] + (1,)))).astype(BF))
    return {"x": f(N, 128, 512), "w": f(N, 128, 4 * NC)}
def setup_inputs_blocks(rng):
    d = setup_inputs(rng)
    for k in ("x", "w"): d[k] = mx_ref.spread(d[k], rng, 4)
    return d
def setup_inputs_wide(rng):
    d = setup_inputs(rng)
    for k in ("x", "w"): d[k] = mx_ref.flush((d[k].astype(np.float32) * np.exp2(rng.integers(-6, 7, (N, 1, 1))).astype(np.float32)).astype(BF))
    return d
def setup_inputs_near(rng):
    d = setup_inputs(rng); v = d["w"].astype(np.float32).reshape(N, 128, -1, 4)
    d["w"] = mx_ref.flush((v[:1, :, :1] + v / 64).reshape(d["w"].shape).astype(BF))
    return d
def setup_inputs_twins(rng):
    d = setup_inputs(rng); v = d["w"].reshape(N, 128, -1, 4).copy(); a, b = rng.permutation(N)[:2]; i, j, k = rng.integers(0, v.shape[2], 3)
    v[a, :, i] = (v[a, :, i].astype(np.float32) * 8).astype(BF); v[a, :, j] = v[a, :, i]; v[b, :, k] = v[a, :, i]
    d["w"] = v.reshape(d["w"].shape)
    return d
def reference(x, w):
    W = [mx_ref.quantize(w[r]) for r in range(N)]
    y = np.zeros((N, 128, 2), np.float32)
    for j in range(N):
        X = mx_ref.quantize(x[j])
        L = np.concatenate([mx_ref.matmul(X, W[r]) for r in range(N)], axis=1)
        y[j][:, 0] = L.max(axis=1); y[j][:, 1] = L.argmax(axis=1)
    return {"y": y}

@@ -1,0 +1,177 @@
+from concourse.bass import DstId, RemoteDMATransfer
+from concourse.mybir import dt, AluOpType, AxisListType, ActivationFunctionType
+
+NCOL = 512
+NEG = -9.0e29
+PLACE = 512
+
+SCRATCH = {
+    "xt": ("sbuf", [128, 512], "bfloat16"),
+    "wt": ("sbuf", [128, 2048], "bfloat16"),
+    "woc": ("sbuf", [128, 512], "float8_e4m3fn_x4"),
+    "wos": ("sbuf", [128, 512], "uint8"),
+    "wnc": ("sbuf", [128, 512], "float8_e4m3fn_x4"),
+    "wns": ("sbuf", [128, 512], "uint8"),
+    "neg": ("sbuf", [128, 512], "float32"),
+    "off": ("sbuf", [128, 8], "float32"),
+    "land": ("sbuf", [128, 16], "float32"),
+    "jj": ("sbuf", [128, 8], "float32"),
+    "ee": ("sbuf", [128, 8], "float32"),
+    "zz": ("sbuf", [128, 16], "float32"),
+    "ps": ("psum", [128, 4096], "float32"),
+}
+for _k in range(4):
+    SCRATCH["xc%d" % _k] = ("sbuf", [128, 128], "float8_e4m3fn_x4")
+    SCRATCH["xs%d" % _k] = ("sbuf", [128, 128], "uint8")
+    SCRATCH["re%d" % _k] = ("sbuf", [128, 512], "float32")
+    SCRATCH["ro%d" % _k] = ("sbuf", [128, 520], "float32")
+    for _b in range(2):
+        SCRATCH["junk%d%d" % (_k, _b)] = ("sbuf", [128, 512], "float32")
+
+SEMAPHORES = ["ldx", "ldwa", "ldwb", "negd", "offd", "qx", "qwa", "qwb", "xsc", "x1", "x2", "x3", "wn",
+              "res", "loc", "own", "f1", "f2", "f3", "fin", "stored"]
+for _k in range(4):
+    SEMAPHORES.append("cp%d" % _k)
+    for _b in range(2):
+        SEMAPHORES += ["mm%d%d" % (_k, _b), "sc%d%d" % (_k, _b), "sg%d%d" % (_k, _b)]
+
+
+def rank_program(g, core, T, topo):
+    rank = T.rank_of(core)
+    if rank is None:
+        return
+    S = T.sem
+    U8 = dt.uint8
+    cores = list(T.cores)
+
+    chips = []
+    for c in cores:
+        if topo.chip(c) not in chips:
+            chips.append(topo.chip(c))
+    members = [[c for c in cores if topo.chip(c) == h] for h in chips]
+    nch = len(chips)
+    a = chips.index(topo.chip(core))
+    b = members[a].index(core)
+    nbr = members[a][1 - b]
+
+    def hops(k):
+        return 1 if all(topo.same_plane(chips[i], chips[(i + k) % nch]) for i in range(nch)) else 2
+    shifts = sorted(range(1, nch), key=lambda k: -hops(k))
+    to = [None] + [members[(a + k) % nch][b] for k in shifts]
+    frm = [None] + [members[(a - k) % nch][b] for k in shifts]
+
+    moff = topo.mask(core, to[1])
+    for k in (2, 3):
+        moff &= topo.mask(core, to[k])
+    mon = topo.mask(core, nbr) & ~moff
+    eoff = bin(moff).count("1")
+    eon = bin(mon).count("1")
+
+    def did(c):
+        rid, pid, _ = topo.addr(c)
+        return DstId(rid=rid, pnc=pid)
+
+    def send(dst, out, in_, sem, mask):
+        rid, pid, _ = topo.addr(dst)
+        g.remote_dma(out, in_, sem, S.loc, pid, rid, mask)
+
+    g.sync.dma_start(T.xt[:], T.x[:]).then_inc(S.ldx, 16)
+    g.sync.dma_start(T.wt[:, 0:1024], T.w[:, 0:1024]).then_inc(S.ldwa, 16)
+    g.sync.dma_start(T.wt[:, 1024:2048], T.w[:, 1024:2048]).then_inc(S.ldwb, 16)
+
+    g.vector.memset(T.neg[:], NEG).then_inc(S.negd, 1)
+    g.vector.wait_ge(S.ldx, 16)
+    g.vector.quantize_mx(T.xc0[:], T.xs0[:], T.xt[:]).then_inc(S.qx, 1)
+    g.vector.wait_ge(S.ldwa, 16)
+    g.vector.quantize_mx(T.woc[:, 0:256], T.wos[:, 0:256], T.wt[:, 0:1024]).then_inc(S.qwa, 1)
+    g.vector.wait_ge(S.ldwb, 16)
+    g.vector.quantize_mx(T.woc[:, 256:512], T.wos[:, 256:512], T.wt[:, 1024:2048]).then_inc(S.qwb, 1)
+
+    g.iota(T.off[:], [[-NCOL, 8]], 7 * NCOL, 0, allow_small_or_imprecise_dtypes=True).then_inc(S.offd, 1)
+    g.wait_ge(S.qx, 1)
+    g.remote_dma_fused([RemoteDMATransfer(
+        dst_ids=[did(to[k]) for k in (1, 2, 3)], dma_engine_mask=moff, remote_sem=S.xsc,
+        srcs=[T.xs0[:]], dsts=[T["xs%d" % k][:] for k in (1, 2, 3)])], local_sem=S.loc)
+    for k in (1, 2, 3):
+        send(to[k], T["xc%d" % k][:].bitcast(U8), T.xc0[:].bitcast(U8), S["x%d" % k], moff)
+    g.wait_ge(S.qwa, 1)
+    send(nbr, T.wnc[:, 0:256].bitcast(U8), T.woc[:, 0:256].bitcast(U8), S.wn, mon)
+    g.wait_ge(S.qwb, 1)
+    send(nbr, T.wnc[:, 256:512].bitcast(U8), T.woc[:, 256:512].bitcast(U8), S.wn, mon)
+    send(nbr, T.wns[:], T.wos[:], S.wn, mon)
+
+    O, F = b, 1 - b
+    order = [(0, O), (1, O), (2, O), (1, F), (2, F), (3, O), (3, F), (0, F)]
+    seen = []
+
+    def once(q, sem, val):
+        if (sem, val) not in seen:
+            seen.append((sem, val))
+            q.wait_ge(S[sem], val)
+
+    for n, (k, p) in enumerate(order):
+        if k == 0:
+            once(g.tensor, "qx", 1)
+        else:
+            once(g.tensor, "xsc", 3 * eoff)
+            once(g.tensor, "x%d" % k, eoff)
+        if p == O:
+            once(g.tensor, "qwa", 1)
+            once(g.tensor, "qwb", 1)
+            wc, ws = T.woc, T.wos
+        else:
+            once(g.tensor, "wn", 3 * eon)
+            wc, ws = T.wnc, T.wns
+        g.tensor.matmul_mx(T.ps[:, NCOL * n:NCOL * (n + 1)], T["xc%d" % k][:], T["xs%d" % k][:], wc[:], ws[:],
+                           True, True).then_inc(S["mm%d%d" % (k, p)], 1)
+
+    def running(k, p):
+        return T["ro%d" % k][:, 1:1 + NCOL] if p else T["re%d" % k][:]
+
+    def last(k, p):
+        return T["ro%d" % k][:, NCOL:NCOL + 1] if p else T["re%d" % k][:, NCOL - 1:NCOL]
+
+    g.vector.wait_ge(S.negd, 1)
+    done = {}
+    for n, (k, p) in enumerate(order):
+        tag = "%d%d" % (k, p)
+        g.vector.wait_ge(S["mm" + tag], 1)
+        g.vector.tensor_tensor_scan(running(k, p), T.neg[:], T.ps[:, NCOL * n:NCOL * (n + 1)], NEG,
+                                    AluOpType.max, AluOpType.max).then_inc(S["sc" + tag], 1)
+        g.scalar.wait_ge(S["sc" + tag], 1)
+        at = PLACE + (1 if p else 3)
+        g.scalar.activation(T["junk" + tag][:], running(k, p), ActivationFunctionType.Sign, bias=last(k, p), scale=-1.0,
+                            accum_out=T["ro%d" % k][:, at:at + 1]).then_inc(S["sg" + tag], 1)
+        done[k] = done.get(k, 0) + 1
+        if done[k] == 2:
+            g.vector.wait_ge(S["sc%d0" % k], 1)
+            g.vector.tensor_copy(T["ro%d" % k][:, PLACE + 2:PLACE + 3], last(k, 0)).then_inc(S["cp%d" % k], 1)
+            if k:
+                g.wait_ge(S["cp%d" % k], 1)
+                g.wait_ge(S["sg%d0" % k], 1)
+                g.wait_ge(S["sg%d1" % k], 1)
+                at = 4 * (nch - 1 - a)
+                send(frm[k], T.land[:, at:at + 4], T["ro%d" % k][:, PLACE:PLACE + 4], S.res, moff)
+
+    g.vector.wait_ge(S.cp0, 1)
+    g.vector.wait_ge(S.sc01, 1)
+    g.vector.wait_ge(S.sg00, 1)
+    g.vector.wait_ge(S.sg01, 1)
+    at = 4 * (nch - 1 - a)
+    g.vector.tensor_copy(T.land[:, at:at + 4], T.ro0[:, PLACE:PLACE + 4]).then_inc(S.own, 1)
+    g.vector.wait_ge(S.offd, 1)
+    g.vector.wait_ge(S.own, 1)
+    g.vector.wait_ge(S.res, 3 * eoff)
+    g.vector.tensor_reduce(T.zz[:, 13:14], T.land[:, 0:16:2], AxisListType.X, AluOpType.max).then_inc(S.f1, 1)
+    g.vector.tensor_tensor(T.jj[:], T.land[:, 1:16:2], T.off[:], AluOpType.add).then_inc(S.f2, 1)
+    g.vector.wait_ge(S.f1, 1)
+    g.vector.tensor_scalar(T.ee[:], T.land[:, 0:16:2], T.zz[:, 13:14], None, AluOpType.is_lt).then_inc(S.f3, 1)
+    g.vector.wait_ge(S.f2, 1)
+    g.vector.wait_ge(S.f3, 1)
+    g.vector.tensor_tensor_scan(T.zz[:, 0:16:2], T.ee[:], T.jj[:], 0.0,
+                                AluOpType.mult, AluOpType.max).then_inc(S.fin, 1)
+    g.sync.wait_ge(S.f1, 1)
+    g.sync.wait_ge(S.fin, 1)
+    g.sync.dma_start(T.y[:], T.zz[:, 13:15]).then_inc(S.stored, 16)
+    g.sync.wait_ge(S.stored, 16)
+    g.wait_ge(S.loc, 4 * eoff + 3 * eon + 3 * eoff)

@@ -3,7 +3,7 @@ from concourse.mybir import dt, AluOpType, AxisListType, ActivationFunctionType
 
 NCOL = 512
 NEG = -9.0e29
-PLACE = 512
+END = 4 * NCOL
 
 SCRATCH = {
     "xt": ("sbuf", [128, 512], "bfloat16"),
@@ -23,15 +23,13 @@ SCRATCH = {
 for _k in range(4):
     SCRATCH["xc%d" % _k] = ("sbuf", [128, 128], "float8_e4m3fn_x4")
     SCRATCH["xs%d" % _k] = ("sbuf", [128, 128], "uint8")
-    SCRATCH["re%d" % _k] = ("sbuf", [128, 512], "float32")
-    SCRATCH["ro%d" % _k] = ("sbuf", [128, 520], "float32")
+    SCRATCH["rr%d" % _k] = ("sbuf", [128, END], "float32")
     for _b in range(2):
         SCRATCH["junk%d%d" % (_k, _b)] = ("sbuf", [128, 512], "float32")
 
 SEMAPHORES = ["ldx", "ldwa", "ldwb", "negd", "offd", "qx", "qwa", "qwb", "xsc", "x1", "x2", "x3", "wn",
               "res", "loc", "own", "f1", "f2", "f3", "fin", "stored"]
 for _k in range(4):
-    SEMAPHORES.append("cp%d" % _k)
     for _b in range(2):
         SEMAPHORES += ["mm%d%d" % (_k, _b), "sc%d%d" % (_k, _b), "sg%d%d" % (_k, _b)]
 
@@ -75,6 +73,9 @@ def rank_program(g, core, T, topo):
         rid, pid, _ = topo.addr(dst)
         g.remote_dma(out, in_, sem, S.loc, pid, rid, mask)
 
+    def codes(k):
+        send(to[k], T["xc%d" % k][:].bitcast(U8), T.xc0[:].bitcast(U8), S["x%d" % k], moff)
+
     g.sync.dma_start(T.xt[:], T.x[:]).then_inc(S.ldx, 16)
     g.sync.dma_start(T.wt[:, 0:1024], T.w[:, 0:1024]).then_inc(S.ldwa, 16)
     g.sync.dma_start(T.wt[:, 1024:2048], T.w[:, 1024:2048]).then_inc(S.ldwb, 16)
@@ -89,11 +90,13 @@ def rank_program(g, core, T, topo):
 
     g.iota(T.off[:], [[-NCOL, 8]], 7 * NCOL, 0, allow_small_or_imprecise_dtypes=True).then_inc(S.offd, 1)
     g.wait_ge(S.qx, 1)
+    send(to[1], T.xs1[:], T.xs0[:], S.x1, moff)
+    codes(1)
     g.remote_dma_fused([RemoteDMATransfer(
-        dst_ids=[did(to[k]) for k in (1, 2, 3)], dma_engine_mask=moff, remote_sem=S.xsc,
-        srcs=[T.xs0[:]], dsts=[T["xs%d" % k][:] for k in (1, 2, 3)])], local_sem=S.loc)
-    for k in (1, 2, 3):
-        send(to[k], T["xc%d" % k][:].bitcast(U8), T.xc0[:].bitcast(U8), S["x%d" % k], moff)
+        dst_ids=[did(to[k]) for k in (2, 3)], dma_engine_mask=moff, remote_sem=S.xsc,
+        srcs=[T.xs0[:]], dsts=[T["xs%d" % k][:] for k in (2, 3)])], local_sem=S.loc)
+    codes(2)
+    codes(3)
     g.wait_ge(S.qwa, 1)
     send(nbr, T.wnc[:, 0:256].bitcast(U8), T.woc[:, 0:256].bitcast(U8), S.wn, mon)
     g.wait_ge(S.qwb, 1)
@@ -101,7 +104,7 @@ def rank_program(g, core, T, topo):
     send(nbr, T.wns[:], T.wos[:], S.wn, mon)
 
     O, F = b, 1 - b
-    order = [(0, O), (1, O), (2, O), (1, F), (2, F), (3, O), (3, F), (0, F)]
+    order = [(0, O), (1, O), (1, F), (2, O), (2, F), (3, O), (3, F), (0, F)]
     seen = []
 
     def once(q, sem, val):
@@ -112,8 +115,10 @@ def rank_program(g, core, T, topo):
     for n, (k, p) in enumerate(order):
         if k == 0:
             once(g.tensor, "qx", 1)
+        elif k == 1:
+            once(g.tensor, "x1", 2 * eoff)
         else:
-            once(g.tensor, "xsc", 3 * eoff)
+            once(g.tensor, "xsc", 2 * eoff)
             once(g.tensor, "x%d" % k, eoff)
         if p == O:
             once(g.tensor, "qwa", 1)
@@ -125,40 +130,33 @@ def rank_program(g, core, T, topo):
         g.tensor.matmul_mx(T.ps[:, NCOL * n:NCOL * (n + 1)], T["xc%d" % k][:], T["xs%d" % k][:], wc[:], ws[:],
                            True, True).then_inc(S["mm%d%d" % (k, p)], 1)
 
-    def running(k, p):
-        return T["ro%d" % k][:, 1:1 + NCOL] if p else T["re%d" % k][:]
-
-    def last(k, p):
-        return T["ro%d" % k][:, NCOL:NCOL + 1] if p else T["re%d" % k][:, NCOL - 1:NCOL]
-
+    at = 4 * (nch - 1 - a)
     g.vector.wait_ge(S.negd, 1)
     done = {}
     for n, (k, p) in enumerate(order):
         tag = "%d%d" % (k, p)
+        rr = T["rr%d" % k]
+        c0 = 0 if p else 2
+        run = rr[:, c0:END:4]
+        m = rr[:, END - 4 + c0:END - 3 + c0]
+        idx = rr[:, END - 3 + c0:END - 2 + c0]
         g.vector.wait_ge(S["mm" + tag], 1)
-        g.vector.tensor_tensor_scan(running(k, p), T.neg[:], T.ps[:, NCOL * n:NCOL * (n + 1)], NEG,
+        g.vector.tensor_tensor_scan(run, T.neg[:], T.ps[:, NCOL * n:NCOL * (n + 1)], NEG,
                                     AluOpType.max, AluOpType.max).then_inc(S["sc" + tag], 1)
         g.scalar.wait_ge(S["sc" + tag], 1)
-        at = PLACE + (1 if p else 3)
-        g.scalar.activation(T["junk" + tag][:], running(k, p), ActivationFunctionType.Sign, bias=last(k, p), scale=-1.0,
-                            accum_out=T["ro%d" % k][:, at:at + 1]).then_inc(S["sg" + tag], 1)
+        g.scalar.activation(T["junk" + tag][:], run, ActivationFunctionType.Sign, bias=m, scale=-1.0,
+                            accum_out=idx).then_inc(S["sg" + tag], 1)
         done[k] = done.get(k, 0) + 1
-        if done[k] == 2:
-            g.vector.wait_ge(S["sc%d0" % k], 1)
-            g.vector.tensor_copy(T["ro%d" % k][:, PLACE + 2:PLACE + 3], last(k, 0)).then_inc(S["cp%d" % k], 1)
-            if k:
-                g.wait_ge(S["cp%d" % k], 1)
-                g.wait_ge(S["sg%d0" % k], 1)
-                g.wait_ge(S["sg%d1" % k], 1)
-                at = 4 * (nch - 1 - a)
-                send(frm[k], T.land[:, at:at + 4], T["ro%d" % k][:, PLACE:PLACE + 4], S.res, moff)
+        if k and done[k] == 2:
+            for q in (0, 1):
+                g.wait_ge(S["sc%d%d" % (k, q)], 1)
+                g.wait_ge(S["sg%d%d" % (k, q)], 1)
+            send(frm[k], T.land[:, at:at + 4], rr[:, END - 4:END], S.res, moff)
 
-    g.vector.wait_ge(S.cp0, 1)
-    g.vector.wait_ge(S.sc01, 1)
-    g.vector.wait_ge(S.sg00, 1)
-    g.vector.wait_ge(S.sg01, 1)
-    at = 4 * (nch - 1 - a)
-    g.vector.tensor_copy(T.land[:, at:at + 4], T.ro0[:, PLACE:PLACE + 4]).then_inc(S.own, 1)
+    for q in (0, 1):
+        g.vector.wait_ge(S["sc0%d" % q], 1)
+        g.vector.wait_ge(S["sg0%d" % q], 1)
+    g.vector.tensor_copy(T.land[:, at:at + 4], T.rr0[:, END - 4:END]).then_inc(S.own, 1)
     g.vector.wait_ge(S.offd, 1)
     g.vector.wait_ge(S.own, 1)
     g.vector.wait_ge(S.res, 3 * eoff)
@@ -170,8 +168,7 @@ def rank_program(g, core, T, topo):
     g.vector.wait_ge(S.f3, 1)
     g.vector.tensor_tensor_scan(T.zz[:, 0:16:2], T.ee[:], T.jj[:], 0.0,
                                 AluOpType.mult, AluOpType.max).then_inc(S.fin, 1)
-    g.sync.wait_ge(S.f1, 1)
     g.sync.wait_ge(S.fin, 1)
     g.sync.dma_start(T.y[:], T.zz[:, 13:15]).then_inc(S.stored, 16)
     g.sync.wait_ge(S.stored, 16)
-    g.wait_ge(S.loc, 4 * eoff + 3 * eon + 3 * eoff)
+    g.wait_ge(S.loc, 5 * eoff + 3 * eon + 3 * eoff)

from concourse.bass import DstId, RemoteDMATransfer
from concourse.mybir import dt, AluOpType, AxisListType, ActivationFunctionType

NCOL = 512
NEG = -9.0e29
END = 4 * NCOL

SCRATCH = {
    "xt": ("sbuf", [128, 512], "bfloat16"),
    "wt": ("sbuf", [128, 2048], "bfloat16"),
    "woc": ("sbuf", [128, 512], "float8_e4m3fn_x4"),
    "wos": ("sbuf", [128, 512], "uint8"),
    "wnc": ("sbuf", [128, 512], "float8_e4m3fn_x4"),
    "wns": ("sbuf", [128, 512], "uint8"),
    "neg": ("sbuf", [128, 512], "float32"),
    "off": ("sbuf", [128, 8], "float32"),
    "land": ("sbuf", [128, 16], "float32"),
    "jj": ("sbuf", [128, 8], "float32"),
    "ee": ("sbuf", [128, 8], "float32"),
    "zz": ("sbuf", [128, 16], "float32"),
    "ps": ("psum", [128, 4096], "float32"),
}
for _k in range(4):
    SCRATCH["xc%d" % _k] = ("sbuf", [128, 128], "float8_e4m3fn_x4")
    SCRATCH["xs%d" % _k] = ("sbuf", [128, 128], "uint8")
    SCRATCH["rr%d" % _k] = ("sbuf", [128, END], "float32")
    for _b in range(2):
        SCRATCH["junk%d%d" % (_k, _b)] = ("sbuf", [128, 512], "float32")

SEMAPHORES = ["ldx", "ldwa", "ldwb", "negd", "offd", "qx", "qwa", "qwb", "xsc", "x1", "x2", "x3", "wn",
              "res", "loc", "own", "f1", "f2", "f3", "fin", "stored"]
for _k in range(4):
    for _b in range(2):
        SEMAPHORES += ["mm%d%d" % (_k, _b), "sc%d%d" % (_k, _b), "sg%d%d" % (_k, _b)]


def rank_program(g, core, T, topo):
    rank = T.rank_of(core)
    if rank is None:
        return
    S = T.sem
    U8 = dt.uint8
    cores = list(T.cores)

    chips = []
    for c in cores:
        if topo.chip(c) not in chips:
            chips.append(topo.chip(c))
    members = [[c for c in cores if topo.chip(c) == h] for h in chips]
    nch = len(chips)
    a = chips.index(topo.chip(core))
    b = members[a].index(core)
    nbr = members[a][1 - b]

    def hops(k):
        return 1 if all(topo.same_plane(chips[i], chips[(i + k) % nch]) for i in range(nch)) else 2
    shifts = sorted(range(1, nch), key=lambda k: -hops(k))
    to = [None] + [members[(a + k) % nch][b] for k in shifts]
    frm = [None] + [members[(a - k) % nch][b] for k in shifts]

    moff = topo.mask(core, to[1])
    for k in (2, 3):
        moff &= topo.mask(core, to[k])
    mon = topo.mask(core, nbr) & ~moff
    eoff = bin(moff).count("1")
    eon = bin(mon).count("1")

    def did(c):
        rid, pid, _ = topo.addr(c)
        return DstId(rid=rid, pnc=pid)

    def send(dst, out, in_, sem, mask):
        rid, pid, _ = topo.addr(dst)
        g.remote_dma(out, in_, sem, S.loc, pid, rid, mask)

    def codes(k):
        send(to[k], T["xc%d" % k][:].bitcast(U8), T.xc0[:].bitcast(U8), S["x%d" % k], moff)

    g.sync.dma_start(T.xt[:], T.x[:]).then_inc(S.ldx, 16)
    g.sync.dma_start(T.wt[:, 0:1024], T.w[:, 0:1024]).then_inc(S.ldwa, 16)
    g.sync.dma_start(T.wt[:, 1024:2048], T.w[:, 1024:2048]).then_inc(S.ldwb, 16)

    g.vector.memset(T.neg[:], NEG).then_inc(S.negd, 1)
    g.vector.wait_ge(S.ldx, 16)
    g.vector.quantize_mx(T.xc0[:], T.xs0[:], T.xt[:]).then_inc(S.qx, 1)
    g.vector.wait_ge(S.ldwa, 16)
    g.vector.quantize_mx(T.woc[:, 0:256], T.wos[:, 0:256], T.wt[:, 0:1024]).then_inc(S.qwa, 1)
    g.vector.wait_ge(S.ldwb, 16)
    g.vector.quantize_mx(T.woc[:, 256:512], T.wos[:, 256:512], T.wt[:, 1024:2048]).then_inc(S.qwb, 1)

    g.iota(T.off[:], [[-NCOL, 8]], 7 * NCOL, 0, allow_small_or_imprecise_dtypes=True).then_inc(S.offd, 1)
    g.wait_ge(S.qx, 1)
    send(to[1], T.xs1[:], T.xs0[:], S.x1, moff)
    codes(1)
    g.remote_dma_fused([RemoteDMATransfer(
        dst_ids=[did(to[k]) for k in (2, 3)], dma_engine_mask=moff, remote_sem=S.xsc,
        srcs=[T.xs0[:]], dsts=[T["xs%d" % k][:] for k in (2, 3)])], local_sem=S.loc)
    codes(2)
    codes(3)
    g.wait_ge(S.qwa, 1)
    send(nbr, T.wnc[:, 0:256].bitcast(U8), T.woc[:, 0:256].bitcast(U8), S.wn, mon)
    g.wait_ge(S.qwb, 1)
    send(nbr, T.wnc[:, 256:512].bitcast(U8), T.woc[:, 256:512].bitcast(U8), S.wn, mon)
    send(nbr, T.wns[:], T.wos[:], S.wn, mon)

    O, F = b, 1 - b
    order = [(0, O), (1, O), (1, F), (2, O), (2, F), (3, O), (3, F), (0, F)]
    seen = []

    def once(q, sem, val):
        if (sem, val) not in seen:
            seen.append((sem, val))
            q.wait_ge(S[sem], val)

    for n, (k, p) in enumerate(order):
        if k == 0:
            once(g.tensor, "qx", 1)
        elif k == 1:
            once(g.tensor, "x1", 2 * eoff)
        else:
            once(g.tensor, "xsc", 2 * eoff)
            once(g.tensor, "x%d" % k, eoff)
        if p == O:
            once(g.tensor, "qwa", 1)
            once(g.tensor, "qwb", 1)
            wc, ws = T.woc, T.wos
        else:
            once(g.tensor, "wn", 3 * eon)
            wc, ws = T.wnc, T.wns
        g.tensor.matmul_mx(T.ps[:, NCOL * n:NCOL * (n + 1)], T["xc%d" % k][:], T["xs%d" % k][:], wc[:], ws[:],
                           True, True).then_inc(S["mm%d%d" % (k, p)], 1)

    at = 4 * (nch - 1 - a)
    g.vector.wait_ge(S.negd, 1)
    done = {}
    for n, (k, p) in enumerate(order):
        tag = "%d%d" % (k, p)
        rr = T["rr%d" % k]
        c0 = 0 if p else 2
        run = rr[:, c0:END:4]
        m = rr[:, END - 4 + c0:END - 3 + c0]
        idx = rr[:, END - 3 + c0:END - 2 + c0]
        g.vector.wait_ge(S["mm" + tag], 1)
        g.vector.tensor_tensor_scan(run, T.neg[:], T.ps[:, NCOL * n:NCOL * (n + 1)], NEG,
                                    AluOpType.max, AluOpType.max).then_inc(S["sc" + tag], 1)
        g.scalar.wait_ge(S["sc" + tag], 1)
        g.scalar.activation(T["junk" + tag][:], run, ActivationFunctionType.Sign, bias=m, scale=-1.0,
                            accum_out=idx).then_inc(S["sg" + tag], 1)
        done[k] = done.get(k, 0) + 1
        if k and done[k] == 2:
            for q in (0, 1):
                g.wait_ge(S["sc%d%d" % (k, q)], 1)
                g.wait_ge(S["sg%d%d" % (k, q)], 1)
            send(frm[k], T.land[:, at:at + 4], rr[:, END - 4:END], S.res, moff)

    for q in (0, 1):
        g.vector.wait_ge(S["sc0%d" % q], 1)
        g.vector.wait_ge(S["sg0%d" % q], 1)
    g.vector.tensor_copy(T.land[:, at:at + 4], T.rr0[:, END - 4:END]).then_inc(S.own, 1)
    g.vector.wait_ge(S.offd, 1)
    g.vector.wait_ge(S.own, 1)
    g.vector.wait_ge(S.res, 3 * eoff)
    g.vector.tensor_reduce(T.zz[:, 13:14], T.land[:, 0:16:2], AxisListType.X, AluOpType.max).then_inc(S.f1, 1)
    g.vector.tensor_tensor(T.jj[:], T.land[:, 1:16:2], T.off[:], AluOpType.add).then_inc(S.f2, 1)
    g.vector.wait_ge(S.f1, 1)
    g.vector.tensor_scalar(T.ee[:], T.land[:, 0:16:2], T.zz[:, 13:14], None, AluOpType.is_lt).then_inc(S.f3, 1)
    g.vector.wait_ge(S.f2, 1)
    g.vector.wait_ge(S.f3, 1)
    g.vector.tensor_tensor_scan(T.zz[:, 0:16:2], T.ee[:], T.jj[:], 0.0,
                                AluOpType.mult, AluOpType.max).then_inc(S.fin, 1)
    g.sync.wait_ge(S.fin, 1)
    g.sync.dma_start(T.y[:], T.zz[:, 13:15]).then_inc(S.stored, 16)
    g.sync.wait_ge(S.stored, 16)
    g.wait_ge(S.loc, 5 * eoff + 3 * eon + 3 * eoff)
